import numpy as np
import ml_dtypes


def mxq(x, axis, fmt="e4m3"):
    dtype, down = {"e4m3": (ml_dtypes.float8_e4m3fn, 7), "e5m2": (ml_dtypes.float8_e5m2, 14)}[fmt]
    v = np.moveaxis(np.asarray(x, np.float32).astype(ml_dtypes.bfloat16).astype(np.float64), axis, -1)
    blocks = v.reshape(v.shape[:-1] + (-1, 32))
    amax = np.abs(blocks).max(-1, keepdims=True)
    byte = np.maximum(np.where(amax > 0, np.frexp(amax)[1] - 1 + 127, 0) - down, 1)
    scale = np.exp2(byte - 127.0)
    codes = (blocks / scale).astype(np.float32).astype(dtype).astype(np.float64)
    return np.moveaxis((codes * scale).reshape(v.shape), -1, axis)


WIDE = False


def mx_kscale(k):
    if not WIDE:
        return np.ones(k)
    levels = np.array([10, -10, 5, -5, 0])
    if k % 512:
        return np.exp2(np.random.permutation(np.resize(levels, k // 32))).repeat(32)
    a = np.empty((k // 512, 16))
    for p in range(k // 512):
        a[p, :8] = np.random.permutation(np.resize(levels, 8))
        for g in range(8):
            far = levels[np.abs(levels - a[p, g]) >= 10]
            a[p, g + 8] = far[np.random.randint(len(far))]
    return np.exp2(a.ravel()).repeat(32)


def f64(x):
    return np.asarray(x).astype(np.float64)


def striped(idx):
    return np.tile(np.asarray(idx).reshape(-1, 16).T, (8, 1)).astype(np.uint16)


def unstriped(offs):
    return offs[:16].T.reshape(-1).astype(np.int64)


E2M1 = np.array([0.0, 0.5, 1.0, 1.5, 2.0, 3.0, 4.0, 6.0, -0.0, -0.5, -1.0, -1.5, -2.0, -3.0, -4.0, -6.0])


def pack_weight(w, fmt):
    k, n = w.shape
    w = f64(np.asarray(w, np.float32).astype(ml_dtypes.bfloat16)).reshape(k // 32, 32, n)
    amax = np.abs(w).max(1)
    if fmt == "e4m3":
        byte = np.frexp(amax)[1] - 1 + 127 - 7
    else:
        mant, ex = np.frexp(amax / 6.0)
        byte = np.where(mant > 0.5, ex, ex - 1) + 127
    byte = np.clip(np.where(amax > 0, byte, 1), 1, 254)
    scaled = (w * np.exp2(127.0 - byte)[:, None, :]).reshape(k, n).astype(np.float32)
    by_word = np.ascontiguousarray(scaled.reshape(k // 512, 128, 4, n).transpose(0, 1, 3, 2))
    if fmt == "e4m3":
        words = by_word.astype(ml_dtypes.float8_e4m3fn).view(np.uint8)
    else:
        c = by_word.astype(ml_dtypes.float4_e2m1fn).view(np.uint8) & 0xF
        words = (c[..., 0::2] | (c[..., 1::2] << 4)).reshape(k // 512, 128, 2 * n)
    return np.ascontiguousarray(words), np.ascontiguousarray(byte.astype(np.uint8).reshape(k // 512, 16, n))


def unpack_weight(words, scales, fmt):
    g, _, n = scales.shape
    words = np.ascontiguousarray(words).reshape(g, 128, n, -1)
    if fmt == "e4m3":
        vals = words.view(ml_dtypes.float8_e4m3fn).astype(np.float64)
    else:
        nib = np.empty((g, 128, n, 4), np.uint8)
        nib[..., 0::2] = words & 0xF
        nib[..., 1::2] = words >> 4
        vals = E2M1[nib]
    vals = vals * np.repeat(np.exp2(scales.astype(np.float64) - 127.0), 8, axis=1)[..., None]
    return vals.transpose(0, 1, 3, 2).reshape(g * 512, n)


B, N, T, D, DV, NQ = 2, 512, 2048, 512, 256, 128
PAGE = 64


def setup_inputs():
    n = np.random.standard_normal
    pages = np.random.permutation(T // PAGE)[:B * N // PAGE]
    idx = (pages[:, None] * PAGE + np.arange(PAGE)[None, :]).reshape(-1)
    s = mx_kscale(D)[:, None]
    u = np.ones(T)
    u[idx] = mx_kscale(B * N)
    r = np.random.uniform(0.5, 2.0, T)
    qp = [pack_weight(x, "e4m3") for x in n((B, D, NQ)) * s * (0.60 / np.sqrt(D))]
    k = n((D, T)) / s
    v = n((DV, T)) / (u * r)
    kp = pack_weight(k, "e4m3")
    return {
        "q_words": np.stack([x[0] for x in qp]),
        "q_scales": np.stack([x[1] for x in qp]),
        "k_words": kp[0],
        "k_scales": kp[1],
        "vT": v.astype(np.float32),
        "vs": np.tile(u * r, (128, 1)).astype(np.float32),
        "offs": striped(idx),
    }


def reference(q_words, q_scales, k_words, k_scales, vT, vs, offs):
    idx = unstriped(offs)
    k = unpack_weight(k_words, k_scales, "e4m3")
    v = f64(vT)
    pick = lambda x: x[:, idx].reshape(x.shape[0], B, N).transpose(1, 0, 2)
    q = np.stack([unpack_weight(q_words[b], q_scales[b], "e4m3") for b in range(B)])
    score = q.transpose(0, 2, 1) @ pick(k)
    p = 1.0 / (1.0 + np.exp(-score))
    w = p * pick(f64(vs))[:, :1, :]
    y = mxq(w, 2, "e4m3") @ mxq(pick(v).transpose(0, 2, 1), 1, "e4m3")
    y = y / 16.0
    return y

@@ -1,0 +1,180 @@
+from contextlib import ExitStack
+
+import concourse.mybir as mybir
+from concourse.masks import make_identity
+
+F32 = mybir.dt.float32
+BF16 = mybir.dt.bfloat16
+I32 = mybir.dt.int32
+U32 = mybir.dt.uint32
+U16 = mybir.dt.uint16
+U8 = mybir.dt.uint8
+FP8X4 = mybir.dt.float8_e4m3fn_x4
+ACT = mybir.ActivationFunctionType
+ALU = mybir.AluOpType
+
+B, N, T, D, DV, NQ = 2, 512, 2048, 512, 256, 128
+P = 128
+PACK = 4
+RUN = 8
+BLOCKS = N // (PACK * RUN)
+LIST_COLS = N // 16
+V_CHUNK = 512
+V_LAST_ON_SCALAR = 192
+
+FLOPS = 2 * B * NQ * N * (D + DV)
+
+
+def dealt(ap):
+    return ap.rearrange("p (r g j) -> p g r j", r=PACK, g=BLOCKS, j=RUN)
+
+
+def tile_attend_qpk_sigmoid_kernel(tc, q_words, q_scales, k_words, k_scales, vT, vs, offs, out):
+    nc = tc.nc
+    with ExitStack() as ctx:
+        keep = ctx.enter_context(tc.tile_pool(name="keep", bufs=1))
+        psum = ctx.enter_context(tc.psum_pool(name="psum", bufs=1))
+
+        offsets = keep.tile([P, B * LIST_COLS], U16, name="offsets")
+        nc.sync.dma_start(offsets[:], offs)
+
+        table_in = keep.tile([P, 1], F32, name="table_in")
+        table_out = keep.tile([P, 1], F32, name="table_out")
+        nc.gpsimd.memset(table_in[:], 0.0)
+        nc.scalar.activation(table_out[:], table_in[:], ACT.Sigmoid)
+
+        vs_pool = keep.tile([P, T], F32, name="vs_pool", align_bytes=64)
+        nc.sync.dma_start(vs_pool[P - 1 : P, :], vs[0:1, :])
+
+        ks_pool = keep.tile([P, T], U8, name="ks_pool", align_bytes=64)
+        nc.vector.memset(ks_pool[:].bitcast(I32), 0)
+        nc.vector.memset(vs_pool[0 : P - 1, 0 : T // 2], 0.0)
+        nc.gpsimd.memset(vs_pool[0 : P - 1, T // 2 : T], 0.0)
+        for quad in range(4):
+            nc.sync.dma_start(
+                ks_pool[32 * quad : 32 * quad + 4, :].bitcast(I32),
+                k_scales[0, 4 * quad : 4 * quad + 4, :].bitcast(I32),
+            )
+
+        v_rows = vT.rearrange("(p j) t -> p j t", j=2)
+        v_raw = []
+        for c in range(T // V_CHUNK):
+            raw = keep.tile([P, 2, V_CHUNK], F32, name=f"v_raw{c}")
+            nc.sync.dma_start(raw[:], v_rows[:, :, c * V_CHUNK : (c + 1) * V_CHUNK])
+            v_raw.append(raw)
+
+        kw_pool = keep.tile([P, T], U32, name="kw_pool", align_bytes=64)
+        nc.sync.dma_start(kw_pool[:].bitcast(I32), k_words[0].rearrange("p t r -> p (t r)").bitcast(I32))
+
+        qw = keep.tile([P, B, NQ], U32, name="qw", align_bytes=64)
+        nc.sync.dma_start(
+            qw[:].bitcast(I32), q_words[:, 0].rearrange("b p q r -> p b (q r)").bitcast(I32)
+        )
+        qs = keep.tile([P, B, NQ], U8, name="qs", align_bytes=64)
+        nc.vector.memset(qs[:].rearrange("p b q -> p (b q)").bitcast(I32), 0)
+        for quad in range(4):
+            nc.sync.dma_start(
+                qs[32 * quad : 32 * quad + 4].bitcast(I32),
+                q_scales[:, 0, 4 * quad : 4 * quad + 4, :].rearrange("b f q -> f b q").bitcast(I32),
+            )
+
+
+        ident = keep.tile([P, P], F32, name="ident", align_bytes=64)
+        make_identity(nc, ident[:])
+
+        def slots(b):
+            return offsets[:, b * LIST_COLS : (b + 1) * LIST_COLS]
+
+        vs_cols = []
+        for b in range(B):
+            vs_listed = keep.tile([P, N], F32, name=f"vs_listed{b}", align_bytes=64)
+            nc.vector.tensor_copy(dealt(vs_listed[:].bitcast(U32)), vs_pool[:].bitcast(U32).indirect(slots(b)))
+            turned = psum.tile([P, PACK, P], F32, name=f"vs_cols{b}")
+            for r in range(PACK):
+                nc.tensor.transpose(turned[:, r, :], vs_listed[:, r * P : (r + 1) * P], ident[:])
+            vs_cols.append(turned)
+
+        ks_listed = keep.tile([P, B * N], U8, name="ks_listed", align_bytes=64)
+        nc.vector.tensor_copy(ks_listed[:], ks_pool[:].indirect(offsets[:]))
+        ks_dealt = keep.tile([P, B * N], U8, name="ks_dealt", align_bytes=64)
+        nc.vector.tensor_copy(
+            ks_dealt[:].bitcast(I32).rearrange("p (b r g w) -> p b r g w", b=B, r=PACK, g=BLOCKS),
+            ks_listed[:].bitcast(I32).rearrange("p (b g r w) -> p b r g w", b=B, r=PACK, g=BLOCKS),
+        )
+
+        v_pool = keep.tile([P, T], U32, name="v_pool", align_bytes=64)
+        v_pairs = v_pool[:].bitcast(BF16).rearrange("p (t j) -> p t j", j=2)
+        last = T // V_CHUNK - 1
+        for c, raw in enumerate(v_raw):
+            t0 = c * V_CHUNK
+            cut = V_CHUNK if c < last else V_LAST_ON_SCALAR
+            nc.scalar.activation(
+                v_pairs[:, t0 : t0 + cut, :], raw[:, :, 0:cut].rearrange("p j t -> p t j"), ACT.Copy
+            )
+            if cut < V_CHUNK:
+                nc.vector.tensor_copy(
+                    v_pairs[:, t0 + cut : t0 + V_CHUNK, :], raw[:, :, cut:V_CHUNK].rearrange("p j t -> p t j")
+                )
+
+        v_grouped = []
+        for b in range(B):
+            v_listed = keep.tile([P, N], U32, name=f"v_listed{b}", align_bytes=64)
+            nc.vector.tensor_copy(dealt(v_listed[:]), v_pool[:].indirect(slots(b)))
+            turned = psum.tile([P, PACK, P], F32, name=f"v_turned{b}")
+            for r in range(PACK):
+                nc.tensor.transpose(turned[:, r, :], v_listed[:, r * P : (r + 1) * P].bitcast(F32), ident[:])
+            grouped = keep.tile([P, DV, PACK], BF16, name=f"v_grouped{b}", align_bytes=64)
+            nc.scalar.copy(grouped[:], turned[:].bitcast(BF16).rearrange("p r e -> p e r"))
+            v_grouped.append(grouped)
+
+        probs = []
+        for b in range(B):
+            kw_listed = keep.tile([P, N], U32, name=f"kw_listed{b}", align_bytes=64)
+            nc.vector.tensor_copy(dealt(kw_listed[:]), kw_pool[:].indirect(slots(b)))
+            scores = psum.tile([P, PACK, NQ], F32, name=f"scores{b}")
+            for r in range(PACK):
+                nc.tensor.matmul_mx(
+                    scores[:, r, :],
+                    lhsT=kw_listed[:, r * P : (r + 1) * P].bitcast(FP8X4),
+                    lhsT_scale=ks_dealt[:, b * N + r * P : b * N + (r + 1) * P],
+                    rhs=qw[:, b, :].bitcast(FP8X4),
+                    rhs_scale=qs[:, b, :],
+                    start=True,
+                    stop=True,
+                )
+            prob = keep.tile([P, NQ, PACK], F32, name=f"prob{b}", align_bytes=64)
+            nc.scalar.activation(prob[:], scores[:].rearrange("p r q -> p q r"), ACT.Sigmoid)
+            probs.append(prob)
+
+        v_codes, v_scales = [], []
+        for b in range(B):
+            codes = keep.tile([P, DV], U32, name=f"v_codes{b}", align_bytes=64)
+            scales = keep.tile([P, DV], U8, name=f"v_scales{b}", align_bytes=64)
+            nc.vector.quantize_mx(codes[:].bitcast(FP8X4), scales[:], v_grouped[b][:].rearrange("p e r -> p (e r)"))
+            v_codes.append(codes)
+            v_scales.append(scales)
+
+        weights = []
+        for b in range(B):
+            w = keep.tile([P, NQ, PACK], BF16, name=f"w{b}", align_bytes=64)
+            scale_by_slot = vs_cols[b][:, :, P - 1 : P].rearrange("p r o -> p o r").broadcast_to([P, NQ, PACK])
+            nc.vector.tensor_tensor(w[:], probs[b][:], scale_by_slot, ALU.mult)
+            weights.append(w)
+
+        for b in range(B):
+            codes = keep.tile([P, NQ], U32, name=f"w_codes{b}", align_bytes=64)
+            scales = keep.tile([P, NQ], U8, name=f"w_scales{b}", align_bytes=64)
+            nc.vector.quantize_mx(codes[:].bitcast(FP8X4), scales[:], weights[b][:].rearrange("p q r -> p (q r)"))
+            y = psum.tile([P, DV], F32, name=f"y{b}")
+            nc.tensor.matmul_mx(
+                y[:],
+                lhsT=codes[:].bitcast(FP8X4),
+                lhsT_scale=scales[:],
+                rhs=v_codes[b][:].bitcast(FP8X4),
+                rhs_scale=v_scales[b][:],
+                start=True,
+                stop=True,
+            )
+            result = keep.tile([P, DV], F32, name=f"result{b}")
+            nc.scalar.activation(result[:], y[:], ACT.Copy, scale=1.0 / 16.0)
+            nc.sync.dma_start(out[b], result[:])

@@ -21,6 +21,7 @@ BLOCKS = N // (PACK * RUN)
 LIST_COLS = N // 16
 V_CHUNK = 512
 V_LAST_ON_SCALAR = 192
+VS_ZERO_SPLIT = 1280
 
 FLOPS = 2 * B * NQ * N * (D + DV)
 
@@ -38,6 +39,9 @@ def tile_attend_qpk_sigmoid_kernel(tc, q_words, q_scales, k_words, k_scales, vT,
         offsets = keep.tile([P, B * LIST_COLS], U16, name="offsets")
         nc.sync.dma_start(offsets[:], offs)
 
+        ks_pool = keep.tile([P, T], U8, name="ks_pool", align_bytes=64)
+        nc.gpsimd.memset(ks_pool[:].bitcast(I32), 0)
+
         table_in = keep.tile([P, 1], F32, name="table_in")
         table_out = keep.tile([P, 1], F32, name="table_out")
         nc.gpsimd.memset(table_in[:], 0.0)
@@ -46,10 +50,8 @@ def tile_attend_qpk_sigmoid_kernel(tc, q_words, q_scales, k_words, k_scales, vT,
         vs_pool = keep.tile([P, T], F32, name="vs_pool", align_bytes=64)
         nc.sync.dma_start(vs_pool[P - 1 : P, :], vs[0:1, :])
 
-        ks_pool = keep.tile([P, T], U8, name="ks_pool", align_bytes=64)
-        nc.vector.memset(ks_pool[:].bitcast(I32), 0)
-        nc.vector.memset(vs_pool[0 : P - 1, 0 : T // 2], 0.0)
-        nc.gpsimd.memset(vs_pool[0 : P - 1, T // 2 : T], 0.0)
+        nc.vector.memset(vs_pool[0 : P - 1, 0:VS_ZERO_SPLIT], 0.0)
+        nc.gpsimd.memset(vs_pool[0 : P - 1, VS_ZERO_SPLIT:T], 0.0)
         for quad in range(4):
             nc.sync.dma_start(
                 ks_pool[32 * quad : 32 * quad + 4, :].bitcast(I32),
@@ -58,29 +60,26 @@ def tile_attend_qpk_sigmoid_kernel(tc, q_words, q_scales, k_words, k_scales, vT,
 
         v_rows = vT.rearrange("(p j) t -> p j t", j=2)
         v_raw = []
+        qw = keep.tile([P, B, NQ], U32, name="qw", align_bytes=64)
+        kw_pool = keep.tile([P, T], U32, name="kw_pool", align_bytes=64)
         for c in range(T // V_CHUNK):
-            raw = keep.tile([P, 2, V_CHUNK], F32, name=f"v_raw{c}")
+            raw = keep.tile([P, 2, V_CHUNK], F32, name=f"v_raw{c}", tag=f"v_raw{c}", align_bytes=64)
             nc.sync.dma_start(raw[:], v_rows[:, :, c * V_CHUNK : (c + 1) * V_CHUNK])
             v_raw.append(raw)
-
-        kw_pool = keep.tile([P, T], U32, name="kw_pool", align_bytes=64)
-        nc.sync.dma_start(kw_pool[:].bitcast(I32), k_words[0].rearrange("p t r -> p (t r)").bitcast(I32))
-
-        qw = keep.tile([P, B, NQ], U32, name="qw", align_bytes=64)
-        nc.sync.dma_start(
-            qw[:].bitcast(I32), q_words[:, 0].rearrange("b p q r -> p b (q r)").bitcast(I32)
-        )
-        qs = keep.tile([P, B, NQ], U8, name="qs", align_bytes=64)
-        nc.vector.memset(qs[:].rearrange("p b q -> p (b q)").bitcast(I32), 0)
-        for quad in range(4):
-            nc.sync.dma_start(
-                qs[32 * quad : 32 * quad + 4].bitcast(I32),
-                q_scales[:, 0, 4 * quad : 4 * quad + 4, :].rearrange("b f q -> f b q").bitcast(I32),
-            )
-
+            if c == 0:
+                nc.sync.dma_start(kw_pool[:].bitcast(I32), k_words[0].rearrange("p t r -> p (t r)").bitcast(I32))
+        nc.sync.dma_start(qw[:].bitcast(I32), q_words[:, 0].rearrange("b p q r -> p b (q r)").bitcast(I32))
 
         ident = keep.tile([P, P], F32, name="ident", align_bytes=64)
         make_identity(nc, ident[:])
+
+        qs = keep.tile([P, B, NQ], U8, name="qs", align_bytes=64)
+        nc.vector.memset(qs[:].rearrange("p b q -> p (b q)").bitcast(I32), 0)
+        for quad in range(4):
+            nc.gpsimd.dma_start(
+                qs[32 * quad : 32 * quad + 4].bitcast(I32),
+                q_scales[:, 0, 4 * quad : 4 * quad + 4, :].rearrange("b f q -> f b q").bitcast(I32),
+            )
 
         def slots(b):
             return offsets[:, b * LIST_COLS : (b + 1) * LIST_COLS]
@@ -116,8 +115,9 @@ def tile_attend_qpk_sigmoid_kernel(tc, q_words, q_scales, k_words, k_scales, vT,
                     v_pairs[:, t0 + cut : t0 + V_CHUNK, :], raw[:, :, cut:V_CHUNK].rearrange("p j t -> p t j")
                 )
 
-        v_grouped = []
-        for b in range(B):
+        prob_both = keep.tile([P, B, NQ, PACK], F32, name="prob_both", tag=f"v_raw{last}", align_bytes=64)
+
+        def values_by_slot(b):
             v_listed = keep.tile([P, N], U32, name=f"v_listed{b}", align_bytes=64)
             nc.vector.tensor_copy(dealt(v_listed[:]), v_pool[:].indirect(slots(b)))
             turned = psum.tile([P, PACK, P], F32, name=f"v_turned{b}")
@@ -125,10 +125,9 @@ def tile_attend_qpk_sigmoid_kernel(tc, q_words, q_scales, k_words, k_scales, vT,
                 nc.tensor.transpose(turned[:, r, :], v_listed[:, r * P : (r + 1) * P].bitcast(F32), ident[:])
             grouped = keep.tile([P, DV, PACK], BF16, name=f"v_grouped{b}", align_bytes=64)
             nc.scalar.copy(grouped[:], turned[:].bitcast(BF16).rearrange("p r e -> p e r"))
-            v_grouped.append(grouped)
+            return grouped
 
-        probs = []
-        for b in range(B):
+        def sigmoid_scores(b):
             kw_listed = keep.tile([P, N], U32, name=f"kw_listed{b}", align_bytes=64)
             nc.vector.tensor_copy(dealt(kw_listed[:]), kw_pool[:].indirect(slots(b)))
             scores = psum.tile([P, PACK, NQ], F32, name=f"scores{b}")
@@ -142,36 +141,34 @@ def tile_attend_qpk_sigmoid_kernel(tc, q_words, q_scales, k_words, k_scales, vT,
                     start=True,
                     stop=True,
                 )
-            prob = keep.tile([P, NQ, PACK], F32, name=f"prob{b}", align_bytes=64)
-            nc.scalar.activation(prob[:], scores[:].rearrange("p r q -> p q r"), ACT.Sigmoid)
-            probs.append(prob)
+            prob = prob_both[:, b]
+            nc.scalar.activation(prob, scores[:].rearrange("p r q -> p q r"), ACT.Sigmoid)
+            return prob
 
-        v_codes, v_scales = [], []
-        for b in range(B):
-            codes = keep.tile([P, DV], U32, name=f"v_codes{b}", align_bytes=64)
-            scales = keep.tile([P, DV], U8, name=f"v_scales{b}", align_bytes=64)
-            nc.vector.quantize_mx(codes[:].bitcast(FP8X4), scales[:], v_grouped[b][:].rearrange("p e r -> p (e r)"))
-            v_codes.append(codes)
-            v_scales.append(scales)
+        def quantised(name, grouped, width):
+            codes = keep.tile([P, width], U32, name=f"{name}_codes", align_bytes=64)
+            scales = keep.tile([P, width], U8, name=f"{name}_scales", align_bytes=64)
+            nc.vector.quantize_mx(codes[:].bitcast(FP8X4), scales[:], grouped)
+            return codes, scales
 
-        weights = []
+        probs = [sigmoid_scores(b) for b in range(B)]
+        v_grouped = [values_by_slot(b) for b in range(B)]
+
+        w = keep.tile([P, B, NQ, PACK], BF16, name="w", align_bytes=64)
         for b in range(B):
-            w = keep.tile([P, NQ, PACK], BF16, name=f"w{b}", align_bytes=64)
             scale_by_slot = vs_cols[b][:, :, P - 1 : P].rearrange("p r o -> p o r").broadcast_to([P, NQ, PACK])
-            nc.vector.tensor_tensor(w[:], probs[b][:], scale_by_slot, ALU.mult)
-            weights.append(w)
+            nc.vector.tensor_tensor(w[:, b], probs[b], scale_by_slot, ALU.mult)
+        w_codes, w_scales = quantised("w", w[:].rearrange("p b q r -> p (b q r)"), B * NQ)
+        v_mx = [quantised(f"v{b}", v_grouped[b][:].rearrange("p e r -> p (e r)"), DV) for b in range(B)]
 
         for b in range(B):
-            codes = keep.tile([P, NQ], U32, name=f"w_codes{b}", align_bytes=64)
-            scales = keep.tile([P, NQ], U8, name=f"w_scales{b}", align_bytes=64)
-            nc.vector.quantize_mx(codes[:].bitcast(FP8X4), scales[:], weights[b][:].rearrange("p q r -> p (q r)"))
             y = psum.tile([P, DV], F32, name=f"y{b}")
             nc.tensor.matmul_mx(
                 y[:],
-                lhsT=codes[:].bitcast(FP8X4),
-                lhsT_scale=scales[:],
-                rhs=v_codes[b][:].bitcast(FP8X4),
-                rhs_scale=v_scales[b][:],
+                lhsT=w_codes[:, b * NQ : (b + 1) * NQ].bitcast(FP8X4),
+                lhsT_scale=w_scales[:, b * NQ : (b + 1) * NQ],
+                rhs=v_mx[b][0][:].bitcast(FP8X4),
+                rhs_scale=v_mx[b][1][:],
                 start=True,
                 stop=True,
             )

@@ -16,18 +16,10 @@ ALU = mybir.AluOpType
 B, N, T, D, DV, NQ = 2, 512, 2048, 512, 256, 128
 P = 128
 PACK = 4
-RUN = 8
-BLOCKS = N // (PACK * RUN)
 LIST_COLS = N // 16
-V_CHUNK = 512
-V_LAST_ON_SCALAR = 192
-VS_ZERO_SPLIT = 1280
+OUT_SCALE = 1.0 / 16.0
 
 FLOPS = 2 * B * NQ * N * (D + DV)
-
-
-def dealt(ap):
-    return ap.rearrange("p (r g j) -> p g r j", r=PACK, g=BLOCKS, j=RUN)
 
 
 def tile_attend_qpk_sigmoid_kernel(tc, q_words, q_scales, k_words, k_scales, vT, vs, offs, out):
@@ -47,34 +39,33 @@ def tile_attend_qpk_sigmoid_kernel(tc, q_words, q_scales, k_words, k_scales, vT,
         nc.gpsimd.memset(table_in[:], 0.0)
         nc.scalar.activation(table_out[:], table_in[:], ACT.Sigmoid)
 
+        qs = keep.tile([P, B, NQ], U8, name="qs", align_bytes=64)
+        nc.vector.memset(qs[:].rearrange("p b q -> p (b q)").bitcast(I32), 0)
+
         vs_pool = keep.tile([P, T], F32, name="vs_pool", align_bytes=64)
         nc.sync.dma_start(vs_pool[P - 1 : P, :], vs[0:1, :])
+        nc.vector.memset(vs_pool[0 : P - 1, :], 0.0)
 
-        nc.vector.memset(vs_pool[0 : P - 1, 0:VS_ZERO_SPLIT], 0.0)
-        nc.gpsimd.memset(vs_pool[0 : P - 1, VS_ZERO_SPLIT:T], 0.0)
         for quad in range(4):
             nc.sync.dma_start(
                 ks_pool[32 * quad : 32 * quad + 4, :].bitcast(I32),
                 k_scales[0, 4 * quad : 4 * quad + 4, :].bitcast(I32),
             )
 
-        v_rows = vT.rearrange("(p j) t -> p j t", j=2)
-        v_raw = []
-        qw = keep.tile([P, B, NQ], U32, name="qw", align_bytes=64)
+        low_raw = []
+        for c in range(2):
+            raw = keep.tile([P, T // 2], F32, name=f"low_raw{c}", tag=f"low_raw{c}", align_bytes=64)
+            nc.sync.dma_start(raw[:], vT[0:P, c * T // 2 : (c + 1) * T // 2])
+            low_raw.append(raw)
         kw_pool = keep.tile([P, T], U32, name="kw_pool", align_bytes=64)
-        for c in range(T // V_CHUNK):
-            raw = keep.tile([P, 2, V_CHUNK], F32, name=f"v_raw{c}", tag=f"v_raw{c}", align_bytes=64)
-            nc.sync.dma_start(raw[:], v_rows[:, :, c * V_CHUNK : (c + 1) * V_CHUNK])
-            v_raw.append(raw)
-            if c == 0:
-                nc.sync.dma_start(kw_pool[:].bitcast(I32), k_words[0].rearrange("p t r -> p (t r)").bitcast(I32))
+        nc.sync.dma_start(kw_pool[:].bitcast(I32), k_words[0].rearrange("p t r -> p (t r)").bitcast(I32))
+        qw = keep.tile([P, B, NQ], U32, name="qw", align_bytes=64)
         nc.sync.dma_start(qw[:].bitcast(I32), q_words[:, 0].rearrange("b p q r -> p b (q r)").bitcast(I32))
+        high_pool = keep.tile([P, T], F32, name="high_pool", tag="high_pool", align_bytes=64)
+        nc.sync.dma_start(high_pool[:], vT[P:DV, :])
 
         ident = keep.tile([P, P], F32, name="ident", align_bytes=64)
         make_identity(nc, ident[:])
-
-        qs = keep.tile([P, B, NQ], U8, name="qs", align_bytes=64)
-        nc.vector.memset(qs[:].rearrange("p b q -> p (b q)").bitcast(I32), 0)
         for quad in range(4):
             nc.gpsimd.dma_start(
                 qs[32 * quad : 32 * quad + 4].bitcast(I32),
@@ -84,94 +75,97 @@ def tile_attend_qpk_sigmoid_kernel(tc, q_words, q_scales, k_words, k_scales, vT,
         def slots(b):
             return offsets[:, b * LIST_COLS : (b + 1) * LIST_COLS]
 
-        vs_cols = []
+        vs_listed = keep.tile([P, B * N], F32, name="vs_listed", align_bytes=64)
+        nc.vector.tensor_copy(vs_listed[:], vs_pool[:].indirect(offsets[:]))
+        vs_turned = []
         for b in range(B):
-            vs_listed = keep.tile([P, N], F32, name=f"vs_listed{b}", align_bytes=64)
-            nc.vector.tensor_copy(dealt(vs_listed[:].bitcast(U32)), vs_pool[:].bitcast(U32).indirect(slots(b)))
-            turned = psum.tile([P, PACK, P], F32, name=f"vs_cols{b}")
+            turned = psum.tile([P, PACK, P], F32, name=f"vs_turned{b}", tag=f"turn{b}")
             for r in range(PACK):
-                nc.tensor.transpose(turned[:, r, :], vs_listed[:, r * P : (r + 1) * P], ident[:])
-            vs_cols.append(turned)
+                nc.tensor.transpose(turned[:, r, :], vs_listed[:, b * N + r : (b + 1) * N : PACK], ident[:])
+            vs_turned.append(turned)
 
         ks_listed = keep.tile([P, B * N], U8, name="ks_listed", align_bytes=64)
         nc.vector.tensor_copy(ks_listed[:], ks_pool[:].indirect(offsets[:]))
-        ks_dealt = keep.tile([P, B * N], U8, name="ks_dealt", align_bytes=64)
-        nc.vector.tensor_copy(
-            ks_dealt[:].bitcast(I32).rearrange("p (b r g w) -> p b r g w", b=B, r=PACK, g=BLOCKS),
-            ks_listed[:].bitcast(I32).rearrange("p (b g r w) -> p b r g w", b=B, r=PACK, g=BLOCKS),
-        )
+        kw_listed = keep.tile([P, B * N], U32, name="kw_listed", align_bytes=64)
+        nc.vector.tensor_copy(kw_listed[:], kw_pool[:].indirect(offsets[:]))
 
-        v_pool = keep.tile([P, T], U32, name="v_pool", align_bytes=64)
-        v_pairs = v_pool[:].bitcast(BF16).rearrange("p (t j) -> p t j", j=2)
-        last = T // V_CHUNK - 1
-        for c, raw in enumerate(v_raw):
-            t0 = c * V_CHUNK
-            cut = V_CHUNK if c < last else V_LAST_ON_SCALAR
-            nc.scalar.activation(
-                v_pairs[:, t0 : t0 + cut, :], raw[:, :, 0:cut].rearrange("p j t -> p t j"), ACT.Copy
+        low_pool = keep.tile([P, T], BF16, name="low_pool", align_bytes=64)
+        for c, raw in enumerate(low_raw):
+            nc.scalar.activation(low_pool[:, c * T // 2 : (c + 1) * T // 2], raw[:], ACT.Copy)
+
+        v_grouped = keep.tile([P, B, DV, PACK], BF16, name="v_grouped", align_bytes=64)
+        v_grouped_words = v_grouped[:].rearrange("p b e t -> p b (e t)").bitcast(F32).rearrange("p b (e u) -> p b e u", u=2)
+
+        def turn_pairs(listed, turned):
+            words = listed[:].bitcast(F32)
+            for u in range(2):
+                nc.tensor.transpose(turned[:, u, :], words[:, u : N // 2 : 2], ident[:])
+
+        low_turned = psum.tile([P, B, 2, P], F32, name="low_turned", tag="low")
+        for b in range(B):
+            listed = keep.tile([P, N], BF16, name=f"low_listed{b}", align_bytes=64)
+            nc.scalar.activation(listed[:], low_pool[:].indirect(slots(b)), ACT.Copy)
+            turn_pairs(listed, low_turned[:, b])
+        vs_cols = keep.tile([P, B, PACK], F32, name="vs_cols", tag="low_raw1", align_bytes=64)
+        for b in range(B):
+            nc.scalar.copy(vs_cols[:, b, :], vs_turned[b][:, :, P - 1])
+        nc.scalar.copy(v_grouped_words[:, :, 0:P, :], low_turned[:].rearrange("p b u e -> p b e u"))
+
+        prob_turned = []
+        for b in range(B):
+            scores = psum.tile([P, N], F32, name=f"scores{b}")
+            nc.tensor.matmul_mx(
+                scores[:],
+                lhsT=qw[:, b, :].bitcast(FP8X4),
+                lhsT_scale=qs[:, b, :],
+                rhs=kw_listed[:, b * N : (b + 1) * N].bitcast(FP8X4),
+                rhs_scale=ks_listed[:, b * N : (b + 1) * N],
+                start=True,
+                stop=True,
             )
-            if cut < V_CHUNK:
-                nc.vector.tensor_copy(
-                    v_pairs[:, t0 + cut : t0 + V_CHUNK, :], raw[:, :, cut:V_CHUNK].rearrange("p j t -> p t j")
-                )
-
-        prob_both = keep.tile([P, B, NQ, PACK], F32, name="prob_both", tag=f"v_raw{last}", align_bytes=64)
-
-        def values_by_slot(b):
-            v_listed = keep.tile([P, N], U32, name=f"v_listed{b}", align_bytes=64)
-            nc.vector.tensor_copy(dealt(v_listed[:]), v_pool[:].indirect(slots(b)))
-            turned = psum.tile([P, PACK, P], F32, name=f"v_turned{b}")
+            prob = keep.tile([P, PACK, P], F32, name=f"prob{b}", align_bytes=64)
+            nc.scalar.activation(prob[:], scores[:].rearrange("p (s r) -> p r s", r=PACK), ACT.Sigmoid)
+            turned = psum.tile([P, PACK, NQ], F32, name=f"prob_turned{b}", tag=f"turn{b}")
             for r in range(PACK):
-                nc.tensor.transpose(turned[:, r, :], v_listed[:, r * P : (r + 1) * P].bitcast(F32), ident[:])
-            grouped = keep.tile([P, DV, PACK], BF16, name=f"v_grouped{b}", align_bytes=64)
-            nc.scalar.copy(grouped[:], turned[:].bitcast(BF16).rearrange("p r e -> p e r"))
-            return grouped
+                nc.tensor.transpose(turned[:, r, :], prob[:, r, :], ident[:])
+            prob_turned.append(turned)
 
-        def sigmoid_scores(b):
-            kw_listed = keep.tile([P, N], U32, name=f"kw_listed{b}", align_bytes=64)
-            nc.vector.tensor_copy(dealt(kw_listed[:]), kw_pool[:].indirect(slots(b)))
-            scores = psum.tile([P, PACK, NQ], F32, name=f"scores{b}")
-            for r in range(PACK):
-                nc.tensor.matmul_mx(
-                    scores[:, r, :],
-                    lhsT=kw_listed[:, r * P : (r + 1) * P].bitcast(FP8X4),
-                    lhsT_scale=ks_dealt[:, b * N + r * P : b * N + (r + 1) * P],
-                    rhs=qw[:, b, :].bitcast(FP8X4),
-                    rhs_scale=qs[:, b, :],
-                    start=True,
-                    stop=True,
-                )
-            prob = prob_both[:, b]
-            nc.scalar.activation(prob, scores[:].rearrange("p r q -> p q r"), ACT.Sigmoid)
-            return prob
+        for b in range(B):
+            listed = keep.tile([P, N], BF16, name=f"high_listed{b}", align_bytes=64)
+            nc.vector.tensor_copy(listed[:], high_pool[:].indirect(slots(b)))
+            turned = psum.tile([P, 2, P], F32, name=f"high_turned{b}")
+            turn_pairs(listed, turned)
+            nc.scalar.copy(v_grouped_words[:, b, P:DV, :], turned[:].rearrange("p u e -> p e u"))
 
-        def quantised(name, grouped, width):
+        def quantised(name, grouped):
+            width = grouped.shape[1] // PACK
             codes = keep.tile([P, width], U32, name=f"{name}_codes", align_bytes=64)
             scales = keep.tile([P, width], U8, name=f"{name}_scales", align_bytes=64)
             nc.vector.quantize_mx(codes[:].bitcast(FP8X4), scales[:], grouped)
             return codes, scales
 
-        probs = [sigmoid_scores(b) for b in range(B)]
-        v_grouped = [values_by_slot(b) for b in range(B)]
-
-        w = keep.tile([P, B, NQ, PACK], BF16, name="w", align_bytes=64)
+        w = keep.tile([P, B, NQ, PACK], BF16, name="w", tag="high_pool", align_bytes=64)
+        half = DV // 2
         for b in range(B):
-            scale_by_slot = vs_cols[b][:, :, P - 1 : P].rearrange("p r o -> p o r").broadcast_to([P, NQ, PACK])
-            nc.vector.tensor_tensor(w[:, b], probs[b], scale_by_slot, ALU.mult)
-        w_codes, w_scales = quantised("w", w[:].rearrange("p b q r -> p (b q r)"), B * NQ)
-        v_mx = [quantised(f"v{b}", v_grouped[b][:].rearrange("p e r -> p (e r)"), DV) for b in range(B)]
-
-        for b in range(B):
-            y = psum.tile([P, DV], F32, name=f"y{b}")
-            nc.tensor.matmul_mx(
-                y[:],
-                lhsT=w_codes[:, b * NQ : (b + 1) * NQ].bitcast(FP8X4),
-                lhsT_scale=w_scales[:, b * NQ : (b + 1) * NQ],
-                rhs=v_mx[b][0][:].bitcast(FP8X4),
-                rhs_scale=v_mx[b][1][:],
-                start=True,
-                stop=True,
-            )
+            scale_by_slot = vs_cols[:, b : b + 1, :].broadcast_to([P, NQ, PACK])
+            nc.vector.tensor_tensor(w[:, b], prob_turned[b][:].rearrange("p r q -> p q r"), scale_by_slot, ALU.mult)
+            v_codes, v_scales = quantised(f"v{b}", v_grouped[:, b].rearrange("p e t -> p (e t)"))
+            w_codes, w_scales = quantised(f"w{b}", w[:, b].rearrange("p q r -> p (q r)"))
             result = keep.tile([P, DV], F32, name=f"result{b}")
-            nc.scalar.activation(result[:], y[:], ACT.Copy, scale=1.0 / 16.0)
+            pieces = [(0, DV, "y")] if b == 0 else [(0, half, "low"), (half, DV, "turn0")]
+            for e0, e1, tag in pieces:
+                y = psum.tile([P, e1 - e0], F32, name=f"y{b}_{e0}", tag=tag)
+                nc.tensor.matmul_mx(
+                    y[:],
+                    lhsT=w_codes[:].bitcast(FP8X4),
+                    lhsT_scale=w_scales[:],
+                    rhs=v_codes[:, e0:e1].bitcast(FP8X4),
+                    rhs_scale=v_scales[:, e0:e1],
+                    start=True,
+                    stop=True,
+                )
+                if e0 == 0:
+                    nc.scalar.activation(result[:, e0:e1], y[:], ACT.Copy, scale=OUT_SCALE)
+                else:
+                    nc.vector.tensor_scalar_mul(result[:, e0:e1], y[:], OUT_SCALE)
             nc.sync.dma_start(out[b], result[:])

@@ -137,9 +137,9 @@ def tile_attend_qpk_sigmoid_kernel(tc, q_words, q_scales, k_words, k_scales, vT,
             turn_pairs(listed, turned)
             nc.scalar.copy(v_grouped_words[:, b, P:DV, :], turned[:].rearrange("p u e -> p e u"))
 
-        def quantised(name, grouped):
+        def quantised(name, grouped, tag):
             width = grouped.shape[1] // PACK
-            codes = keep.tile([P, width], U32, name=f"{name}_codes", align_bytes=64)
+            codes = keep.tile([P, width], U32, name=f"{name}_codes", tag=tag, align_bytes=64)
             scales = keep.tile([P, width], U8, name=f"{name}_scales", align_bytes=64)
             nc.vector.quantize_mx(codes[:].bitcast(FP8X4), scales[:], grouped)
             return codes, scales
@@ -149,8 +149,8 @@ def tile_attend_qpk_sigmoid_kernel(tc, q_words, q_scales, k_words, k_scales, vT,
         for b in range(B):
             scale_by_slot = vs_cols[:, b : b + 1, :].broadcast_to([P, NQ, PACK])
             nc.vector.tensor_tensor(w[:, b], prob_turned[b][:].rearrange("p r q -> p q r"), scale_by_slot, ALU.mult)
-            v_codes, v_scales = quantised(f"v{b}", v_grouped[:, b].rearrange("p e t -> p (e t)"))
-            w_codes, w_scales = quantised(f"w{b}", w[:, b].rearrange("p q r -> p (q r)"))
+            v_codes, v_scales = quantised(f"v{b}", v_grouped[:, b].rearrange("p e t -> p (e t)"), ("v0_codes", "low_raw1")[b])
+            w_codes, w_scales = quantised(f"w{b}", w[:, b].rearrange("p q r -> p (q r)"), f"w{b}_codes")
             result = keep.tile([P, DV], F32, name=f"result{b}")
             pieces = [(0, DV, "y")] if b == 0 else [(0, half, "low"), (half, DV, "turn0")]
             for e0, e1, tag in pieces:

from contextlib import ExitStack

import concourse.mybir as mybir
from concourse.masks import make_identity

F32 = mybir.dt.float32
BF16 = mybir.dt.bfloat16
I32 = mybir.dt.int32
U32 = mybir.dt.uint32
U16 = mybir.dt.uint16
U8 = mybir.dt.uint8
FP8X4 = mybir.dt.float8_e4m3fn_x4
ACT = mybir.ActivationFunctionType
ALU = mybir.AluOpType

B, N, T, D, DV, NQ = 2, 512, 2048, 512, 256, 128
P = 128
PACK = 4
LIST_COLS = N // 16
OUT_SCALE = 1.0 / 16.0

FLOPS = 2 * B * NQ * N * (D + DV)


def tile_attend_qpk_sigmoid_kernel(tc, q_words, q_scales, k_words, k_scales, vT, vs, offs, out):
    nc = tc.nc
    with ExitStack() as ctx:
        keep = ctx.enter_context(tc.tile_pool(name="keep", bufs=1))
        psum = ctx.enter_context(tc.psum_pool(name="psum", bufs=1))

        offsets = keep.tile([P, B * LIST_COLS], U16, name="offsets")
        nc.sync.dma_start(offsets[:], offs)

        ks_pool = keep.tile([P, T], U8, name="ks_pool", align_bytes=64)
        nc.gpsimd.memset(ks_pool[:].bitcast(I32), 0)

        table_in = keep.tile([P, 1], F32, name="table_in")
        table_out = keep.tile([P, 1], F32, name="table_out")
        nc.gpsimd.memset(table_in[:], 0.0)
        nc.scalar.activation(table_out[:], table_in[:], ACT.Sigmoid)

        qs = keep.tile([P, B, NQ], U8, name="qs", align_bytes=64)
        nc.vector.memset(qs[:].rearrange("p b q -> p (b q)").bitcast(I32), 0)

        vs_pool = keep.tile([P, T], F32, name="vs_pool", align_bytes=64)
        nc.sync.dma_start(vs_pool[P - 1 : P, :], vs[0:1, :])
        nc.vector.memset(vs_pool[0 : P - 1, :], 0.0)

        for quad in range(4):
            nc.sync.dma_start(
                ks_pool[32 * quad : 32 * quad + 4, :].bitcast(I32),
                k_scales[0, 4 * quad : 4 * quad + 4, :].bitcast(I32),
            )

        low_raw = []
        for c in range(2):
            raw = keep.tile([P, T // 2], F32, name=f"low_raw{c}", tag=f"low_raw{c}", align_bytes=64)
            nc.sync.dma_start(raw[:], vT[0:P, c * T // 2 : (c + 1) * T // 2])
            low_raw.append(raw)
        kw_pool = keep.tile([P, T], U32, name="kw_pool", align_bytes=64)
        nc.sync.dma_start(kw_pool[:].bitcast(I32), k_words[0].rearrange("p t r -> p (t r)").bitcast(I32))
        qw = keep.tile([P, B, NQ], U32, name="qw", align_bytes=64)
        nc.sync.dma_start(qw[:].bitcast(I32), q_words[:, 0].rearrange("b p q r -> p b (q r)").bitcast(I32))
        high_pool = keep.tile([P, T], F32, name="high_pool", tag="high_pool", align_bytes=64)
        nc.sync.dma_start(high_pool[:], vT[P:DV, :])

        ident = keep.tile([P, P], F32, name="ident", align_bytes=64)
        make_identity(nc, ident[:])
        for quad in range(4):
            nc.gpsimd.dma_start(
                qs[32 * quad : 32 * quad + 4].bitcast(I32),
                q_scales[:, 0, 4 * quad : 4 * quad + 4, :].rearrange("b f q -> f b q").bitcast(I32),
            )

        def slots(b):
            return offsets[:, b * LIST_COLS : (b + 1) * LIST_COLS]

        vs_listed = keep.tile([P, B * N], F32, name="vs_listed", align_bytes=64)
        nc.vector.tensor_copy(vs_listed[:], vs_pool[:].indirect(offsets[:]))
        vs_turned = []
        for b in range(B):
            turned = psum.tile([P, PACK, P], F32, name=f"vs_turned{b}", tag=f"turn{b}")
            for r in range(PACK):
                nc.tensor.transpose(turned[:, r, :], vs_listed[:, b * N + r : (b + 1) * N : PACK], ident[:])
            vs_turned.append(turned)

        ks_listed = keep.tile([P, B * N], U8, name="ks_listed", align_bytes=64)
        nc.vector.tensor_copy(ks_listed[:], ks_pool[:].indirect(offsets[:]))
        kw_listed = keep.tile([P, B * N], U32, name="kw_listed", align_bytes=64)
        nc.vector.tensor_copy(kw_listed[:], kw_pool[:].indirect(offsets[:]))

        low_pool = keep.tile([P, T], BF16, name="low_pool", align_bytes=64)
        for c, raw in enumerate(low_raw):
            nc.scalar.activation(low_pool[:, c * T // 2 : (c + 1) * T // 2], raw[:], ACT.Copy)

        v_grouped = keep.tile([P, B, DV, PACK], BF16, name="v_grouped", align_bytes=64)
        v_grouped_words = v_grouped[:].rearrange("p b e t -> p b (e t)").bitcast(F32).rearrange("p b (e u) -> p b e u", u=2)

        def turn_pairs(listed, turned):
            words = listed[:].bitcast(F32)
            for u in range(2):
                nc.tensor.transpose(turned[:, u, :], words[:, u : N // 2 : 2], ident[:])

        low_turned = psum.tile([P, B, 2, P], F32, name="low_turned", tag="low")
        for b in range(B):
            listed = keep.tile([P, N], BF16, name=f"low_listed{b}", align_bytes=64)
            nc.scalar.activation(listed[:], low_pool[:].indirect(slots(b)), ACT.Copy)
            turn_pairs(listed, low_turned[:, b])
        vs_cols = keep.tile([P, B, PACK], F32, name="vs_cols", tag="low_raw1", align_bytes=64)
        for b in range(B):
            nc.scalar.copy(vs_cols[:, b, :], vs_turned[b][:, :, P - 1])
        nc.scalar.copy(v_grouped_words[:, :, 0:P, :], low_turned[:].rearrange("p b u e -> p b e u"))

        prob_turned = []
        for b in range(B):
            scores = psum.tile([P, N], F32, name=f"scores{b}")
            nc.tensor.matmul_mx(
                scores[:],
                lhsT=qw[:, b, :].bitcast(FP8X4),
                lhsT_scale=qs[:, b, :],
                rhs=kw_listed[:, b * N : (b + 1) * N].bitcast(FP8X4),
                rhs_scale=ks_listed[:, b * N : (b + 1) * N],
                start=True,
                stop=True,
            )
            prob = keep.tile([P, PACK, P], F32, name=f"prob{b}", align_bytes=64)
            nc.scalar.activation(prob[:], scores[:].rearrange("p (s r) -> p r s", r=PACK), ACT.Sigmoid)
            turned = psum.tile([P, PACK, NQ], F32, name=f"prob_turned{b}", tag=f"turn{b}")
            for r in range(PACK):
                nc.tensor.transpose(turned[:, r, :], prob[:, r, :], ident[:])
            prob_turned.append(turned)

        for b in range(B):
            listed = keep.tile([P, N], BF16, name=f"high_listed{b}", align_bytes=64)
            nc.vector.tensor_copy(listed[:], high_pool[:].indirect(slots(b)))
            turned = psum.tile([P, 2, P], F32, name=f"high_turned{b}")
            turn_pairs(listed, turned)
            nc.scalar.copy(v_grouped_words[:, b, P:DV, :], turned[:].rearrange("p u e -> p e u"))

        def quantised(name, grouped, tag):
            width = grouped.shape[1] // PACK
            codes = keep.tile([P, width], U32, name=f"{name}_codes", tag=tag, align_bytes=64)
            scales = keep.tile([P, width], U8, name=f"{name}_scales", align_bytes=64)
            nc.vector.quantize_mx(codes[:].bitcast(FP8X4), scales[:], grouped)
            return codes, scales

        w = keep.tile([P, B, NQ, PACK], BF16, name="w", tag="high_pool", align_bytes=64)
        half = DV // 2
        for b in range(B):
            scale_by_slot = vs_cols[:, b : b + 1, :].broadcast_to([P, NQ, PACK])
            nc.vector.tensor_tensor(w[:, b], prob_turned[b][:].rearrange("p r q -> p q r"), scale_by_slot, ALU.mult)
            v_codes, v_scales = quantised(f"v{b}", v_grouped[:, b].rearrange("p e t -> p (e t)"), ("v0_codes", "low_raw1")[b])
            w_codes, w_scales = quantised(f"w{b}", w[:, b].rearrange("p q r -> p (q r)"), f"w{b}_codes")
            result = keep.tile([P, DV], F32, name=f"result{b}")
            pieces = [(0, DV, "y")] if b == 0 else [(0, half, "low"), (half, DV, "turn0")]
            for e0, e1, tag in pieces:
                y = psum.tile([P, e1 - e0], F32, name=f"y{b}_{e0}", tag=tag)
                nc.tensor.matmul_mx(
                    y[:],
                    lhsT=w_codes[:].bitcast(FP8X4),
                    lhsT_scale=w_scales[:],
                    rhs=v_codes[:, e0:e1].bitcast(FP8X4),
                    rhs_scale=v_scales[:, e0:e1],
                    start=True,
                    stop=True,
                )
                if e0 == 0:
                    nc.scalar.activation(result[:, e0:e1], y[:], ACT.Copy, scale=OUT_SCALE)
                else:
                    nc.vector.tensor_scalar_mul(result[:, e0:e1], y[:], OUT_SCALE)
            nc.sync.dma_start(out[b], result[:])
